import numpy as np
import ml_dtypes


def mxq(x, axis, fmt="e4m3"):
    dtype, down = {"e4m3": (ml_dtypes.float8_e4m3fn, 7), "e5m2": (ml_dtypes.float8_e5m2, 14)}[fmt]
    v = np.moveaxis(np.asarray(x, np.float32).astype(ml_dtypes.bfloat16).astype(np.float64), axis, -1)
    blocks = v.reshape(v.shape[:-1] + (-1, 32))
    amax = np.abs(blocks).max(-1, keepdims=True)
    byte = np.maximum(np.where(amax > 0, np.frexp(amax)[1] - 1 + 127, 0) - down, 1)
    scale = np.exp2(byte - 127.0)
    codes = (blocks / scale).astype(np.float32).astype(dtype).astype(np.float64)
    return np.moveaxis((codes * scale).reshape(v.shape), -1, axis)


WIDE = False


def mx_kscale(k):
    if not WIDE:
        return np.ones(k)
    levels = np.array([10, -10, 5, -5, 0])
    if k % 512:
        return np.exp2(np.random.permutation(np.resize(levels, k // 32))).repeat(32)
    a = np.empty((k // 512, 16))
    for p in range(k // 512):
        a[p, :8] = np.random.permutation(np.resize(levels, 8))
        for g in range(8):
            far = levels[np.abs(levels - a[p, g]) >= 10]
            a[p, g + 8] = far[np.random.randint(len(far))]
    return np.exp2(a.ravel()).repeat(32)


BF16 = ml_dtypes.bfloat16


def bf(x):
    return np.asarray(x, np.float32).astype(BF16)


def f64(x):
    return np.asarray(x).astype(np.float64)


E2M1 = np.array([0.0, 0.5, 1.0, 1.5, 2.0, 3.0, 4.0, 6.0, -0.0, -0.5, -1.0, -1.5, -2.0, -3.0, -4.0, -6.0])


def pack_weight(w, fmt):
    k, n = w.shape
    w = f64(bf(w)).reshape(k // 32, 32, n)
    amax = np.abs(w).max(1)
    if fmt == "e4m3":
        byte = np.frexp(amax)[1] - 1 + 127 - 7
    else:
        mant, ex = np.frexp(amax / 6.0)
        byte = np.where(mant > 0.5, ex, ex - 1) + 127
    byte = np.clip(np.where(amax > 0, byte, 1), 1, 254)
    scaled = (w * np.exp2(127.0 - byte)[:, None, :]).reshape(k, n).astype(np.float32)
    by_word = np.ascontiguousarray(scaled.reshape(k // 512, 128, 4, n).transpose(0, 1, 3, 2))
    if fmt == "e4m3":
        words = by_word.astype(ml_dtypes.float8_e4m3fn).view(np.uint8)
    else:
        c = by_word.astype(ml_dtypes.float4_e2m1fn).view(np.uint8) & 0xF
        words = c[..., 0::2] | (c[..., 1::2] << 4)
    return np.ascontiguousarray(words), np.ascontiguousarray(byte.astype(np.uint8).reshape(k // 512, 16, n))


def unpack_weight(words, scales, fmt):
    g, p, n, _ = words.shape
    if fmt == "e4m3":
        vals = np.ascontiguousarray(words).view(ml_dtypes.float8_e4m3fn).astype(np.float64)
    else:
        nib = np.empty((g, p, n, 4), np.uint8)
        nib[..., 0::2] = words & 0xF
        nib[..., 1::2] = words >> 4
        vals = E2M1[nib]
    vals = vals * np.repeat(np.exp2(scales.astype(np.float64) - 127.0), 8, axis=1)[..., None]
    return vals.transpose(0, 1, 3, 2).reshape(g * 512, n)
def pack4(w):
    words, scales = pack_weight(w, "e2m1")
    return words.reshape(words.shape[0], 128, -1), scales


def unpack4(words, scales):
    return unpack_weight(words.reshape(words.shape[0], 128, -1, 2), scales, "e2m1")


M, N = 512, 1536

RELAXED = 0.35
OFFSET = 0.25


def setup_inputs():
    s = mx_kscale(N)
    x0 = np.random.standard_normal((M, N)) * s
    c1 = OFFSET * np.random.standard_normal((M, N)) * s
    c2 = OFFSET * np.random.standard_normal((M, N)) * s
    d = (1 + 0.1 * np.random.standard_normal(N)) / s
    p1 = RELAXED * np.random.standard_normal((N, N)) / np.sqrt(N) / s[:, None] * s
    p2 = RELAXED * np.random.standard_normal((N, N)) / np.sqrt(N) / s[:, None] * s
    p3 = RELAXED * np.random.standard_normal((N, N)) / np.sqrt(N) / s[:, None] * s
    proj1_words, proj1_scales = pack4(p1)
    proj2_words, proj2_scales = pack4(p2)
    proj3_words, proj3_scales = pack4(p3)
    return {"x0": bf(x0), "c1": bf(c1), "c2": bf(c2), "d": bf(d),
            "proj1_words": proj1_words, "proj1_scales": proj1_scales,
            "proj2_words": proj2_words, "proj2_scales": proj2_scales,
            "proj3_words": proj3_words, "proj3_scales": proj3_scales}


def reference(x0, c1, c2, d, proj1_words, proj1_scales, proj2_words, proj2_scales, proj3_words, proj3_scales):
    x = f64(x0)
    x1 = x - (mxq(x, 1, "e4m3") @ unpack4(proj1_words, proj1_scales)) + f64(c1)
    x2 = x1 - (mxq(x1, 1, "e4m3") @ unpack4(proj2_words, proj2_scales)) + f64(c2)
    x3 = x2 - (mxq(x2, 1, "e4m3") @ unpack4(proj3_words, proj3_scales))
    return x3 * f64(d)

@@ -1,0 +1,175 @@
+from contextlib import ExitStack
+
+import concourse.mybir as mybir
+from concourse.masks import make_identity
+
+M, N = 512, 1536
+FLOPS = 3 * 2 * M * N * N
+
+F32 = mybir.dt.float32
+BF16 = mybir.dt.bfloat16
+I32 = mybir.dt.int32
+U32 = mybir.dt.uint32
+U8 = mybir.dt.uint8
+FP8X4 = mybir.dt.float8_e4m3fn_x4
+FP4X4 = mybir.dt.float4_e2m1fn_x4
+ALU = mybir.AluOpType
+
+P = 128
+CHUNK = 512
+GROUPS = N // CHUNK
+TILES = M // P
+STAGES = 3
+STEPS = STAGES * TILES
+PARTS = ((0, 1), (1, 2))
+
+
+def tile_block_kaczmarz_sweep_t2_kernel(
+    tc, x0, c1, c2, d, proj1_words, proj1_scales, proj2_words, proj2_scales, proj3_words, proj3_scales, out
+):
+    nc = tc.nc
+    words_hbm = (proj1_words, proj2_words, proj3_words)
+    scales_hbm = (proj1_scales, proj2_scales, proj3_scales)
+
+    with ExitStack() as ctx:
+        keep = ctx.enter_context(tc.tile_pool(name="keep", bufs=1))
+        work = ctx.enter_context(tc.tile_pool(name="work", bufs=3))
+        psum = ctx.enter_context(tc.psum_pool(name="psum", bufs=1))
+        ctx.enter_context(tc.manual_schedule())
+
+        identity = keep.tile([P, P], F32, name="identity")
+        make_identity(nc, identity[:])
+
+        w_scales = []
+        for s in range(STAGES):
+            plane = keep.tile([P, GROUPS, N], U8, name="w_scales%d" % s, align_bytes=64)
+            nc.vector.memset(plane[:].bitcast(I32), 0)
+            w_scales.append(plane)
+
+        def load_rows(src, m, label):
+            t = keep.tile([P, N], BF16, name="%s%d" % (label, m))
+            nc.sync.dma_start(out=t[:], in_=src[m * P : (m + 1) * P, :])
+            return t
+
+        def load_words(s, g):
+            t = keep.tile([P, 2 * N], U8, name="w_words%d_%d" % (s, g), align_bytes=64)
+            nc.sync.dma_start(out=t[:].bitcast(I32), in_=words_hbm[s][g].bitcast(I32))
+            return t
+
+        def load_scales(s):
+            rows = scales_hbm[s].bitcast(I32).rearrange("g (q r) n -> r q g n", r=4)
+            for r in range(4):
+                nc.sync.dma_start(out=w_scales[s][:].bitcast(I32)[r:P:32], in_=rows[r])
+
+        x0_t, c1_t, c2_t, w_words = {}, {}, {}, {}
+        x0_t[0] = load_rows(x0, 0, "x0_")
+        w_words[0, 0] = load_words(0, 0)
+        load_scales(0)
+        x0_t[1] = load_rows(x0, 1, "x0_")
+        w_words[0, 1] = load_words(0, 1)
+        w_words[0, 2] = load_words(0, 2)
+        for m in range(TILES):
+            c1_t[m] = load_rows(c1, m, "c1_")
+            if m + 2 < TILES:
+                x0_t[m + 2] = load_rows(x0, m + 2, "x0_")
+        load_scales(1)
+        for g in range(GROUPS):
+            w_words[1, g] = load_words(1, g)
+        for m in range(TILES):
+            c2_t[m] = load_rows(c2, m, "c2_")
+        load_scales(2)
+        for g in range(GROUPS):
+            w_words[2, g] = load_words(2, g)
+        d_t = keep.tile([P, N], BF16, name="d_t")
+        nc.sync.dma_start(out=d_t[:], in_=d.partition_broadcast(P))
+
+        rounded, grouped, codes, scales, x_t = {}, {}, {}, {}, {}
+
+        def turn(j):
+            for part, (g0, ng) in enumerate(PARTS):
+                bank = psum.tile([P, ng, 2, P], F32, name="turn%d" % part)
+                for gl in range(ng):
+                    for u in range(2):
+                        if j < TILES:
+                            base = 256 * (g0 + gl)
+                            src = x0_t[j][:].bitcast(F32)[:, base + u : base + 256 : 2]
+                        else:
+                            base = 256 * gl + P * u
+                            src = rounded[j, part][:].bitcast(F32)[:, base : base + P]
+                        nc.tensor.transpose(bank[:, gl, u, :], src, identity[:])
+                t = work.tile([P, ng * CHUNK], BF16, name="grouped%d" % part, align_bytes=64)
+                nc.scalar.copy(
+                    out=t[:].bitcast(F32).rearrange("p (g m u) -> p g m u", g=ng, u=2),
+                    in_=bank[:].rearrange("p g u m -> p g m u"),
+                )
+                grouped[j, part] = t
+
+        def quantize(j):
+            for part, (g0, ng) in enumerate(PARTS):
+                cw = work.tile([P, ng * P], U32, name="codes%d" % part, align_bytes=64)
+                sc = work.tile([P, ng * P], U8, name="scales%d" % part, align_bytes=64)
+                nc.vector.quantize_mx(out=cw[:].bitcast(FP8X4), scales=sc[:], in_=grouped[j, part][:])
+                for gl in range(ng):
+                    codes[j, g0 + gl] = cw[:, gl * P : (gl + 1) * P]
+                    scales[j, g0 + gl] = sc[:, gl * P : (gl + 1) * P]
+
+        def mx_pass(i, acc, ch, g):
+            s = i // TILES
+            nc.tensor.matmul_mx(
+                out=acc[:],
+                lhsT=codes[i, g].bitcast(FP8X4),
+                lhsT_scale=scales[i, g],
+                rhs=w_words[s, g][:, 2 * ch * CHUNK : 2 * (ch + 1) * CHUNK].bitcast(FP4X4),
+                rhs_scale=w_scales[s][:, g, ch * CHUNK : (ch + 1) * CHUNK],
+                start=(g == 0),
+                stop=(g == GROUPS - 1),
+            )
+
+        turn(0)
+        quantize(0)
+        for i in range(STEPS):
+            s, m = divmod(i, TILES)
+            accs = []
+            for ch in range(GROUPS):
+                acc = psum.tile([P, CHUNK], F32, name="acc", bufs=6)
+                accs.append(acc)
+            first = 0
+            if i == 0:
+                for ch in range(GROUPS):
+                    mx_pass(i, accs[ch], ch, 0)
+                turn(1)
+                quantize(1)
+                first = 1
+            for ch in range(GROUPS):
+                for g in range(first, GROUPS):
+                    mx_pass(i, accs[ch], ch, g)
+            if i + 2 < STEPS:
+                turn(i + 2)
+
+            minuend = (c1_t[m], c2_t[m], x_t.get(i - TILES))[s]
+            other = (x0_t[m], x_t.get(i - TILES), d_t)[s]
+            op = ALU.mult if s == STAGES - 1 else ALU.add
+            diff = work.tile([P, N], F32, name="diff")
+            res = keep.tile([P, N], F32, name="res%d" % i)
+            x_t[i] = res
+            for ch in range(GROUPS):
+                cols = slice(ch * CHUNK, (ch + 1) * CHUNK)
+                nc.vector.tensor_tensor(out=diff[:, cols], in0=minuend[:, cols], in1=accs[ch][:], op=ALU.subtract)
+            for ch in range(GROUPS):
+                cols = slice(ch * CHUNK, (ch + 1) * CHUNK)
+                eng = nc.gpsimd if ch == 0 else nc.vector
+                eng.tensor_tensor(out=res[:, cols], in0=diff[:, cols], in1=other[:, cols], op=op)
+                if s == STAGES - 1:
+                    nc.sync.dma_start(out=out[m * P : (m + 1) * P, cols], in_=res[:, cols])
+            if i + 2 < STEPS:
+                quantize(i + 2)
+            if s < STAGES - 1:
+                for part, (g0, ng) in enumerate(PARTS):
+                    t = work.tile([P, ng * CHUNK], BF16, name="rounded%d" % part)
+                    nc.scalar.copy(
+                        out=t[:].rearrange("p (g u q e) -> p g u q e", g=ng, u=2, e=2),
+                        in_=res[:, g0 * CHUNK : (g0 + ng) * CHUNK].rearrange(
+                            "p (g q u e) -> p g u q e", g=ng, u=2, e=2
+                        ),
+                    )
+                    rounded[i + TILES, part] = t

@@ -22,6 +22,8 @@ TILES = M // P
 STAGES = 3
 STEPS = STAGES * TILES
 PARTS = ((0, 1), (1, 2))
+D_SPLIT = 768
+D_ROWS = (N - D_SPLIT) // P
 
 
 def tile_block_kaczmarz_sweep_t2_kernel(
@@ -46,14 +48,20 @@ def tile_block_kaczmarz_sweep_t2_kernel(
             nc.vector.memset(plane[:].bitcast(I32), 0)
             w_scales.append(plane)
 
+        identity_bf = keep.tile([P, P], BF16, name="identity_bf")
+        nc.scalar.copy(out=identity_bf[:], in_=identity[:])
+        d_rows = keep.tile([P, P], BF16, name="d_rows")
+        nc.vector.memset(d_rows[:], 0.0)
+
         def load_rows(src, m, label):
             t = keep.tile([P, N], BF16, name="%s%d" % (label, m))
             nc.sync.dma_start(out=t[:], in_=src[m * P : (m + 1) * P, :])
             return t
 
-        def load_words(s, g):
-            t = keep.tile([P, 2 * N], U8, name="w_words%d_%d" % (s, g), align_bytes=64)
-            nc.sync.dma_start(out=t[:].bitcast(I32), in_=words_hbm[s][g].bitcast(I32))
+        def load_words(s, ch):
+            t = keep.tile([P, GROUPS, 2 * CHUNK], U8, name="w_words%d_%d" % (s, ch), align_bytes=64)
+            src = words_hbm[s].bitcast(I32).rearrange("g p n -> p g n")
+            nc.sync.dma_start(out=t[:].bitcast(I32), in_=src[:, :, ch * CHUNK // 2 : (ch + 1) * CHUNK // 2])
             return t
 
         def load_scales(s):
@@ -66,12 +74,14 @@ def tile_block_kaczmarz_sweep_t2_kernel(
         w_words[0, 0] = load_words(0, 0)
         load_scales(0)
         x0_t[1] = load_rows(x0, 1, "x0_")
+        c1_t[0] = load_rows(c1, 0, "c1_")
         w_words[0, 1] = load_words(0, 1)
         w_words[0, 2] = load_words(0, 2)
-        for m in range(TILES):
+        for m in range(1, TILES):
+            if m + 1 < TILES:
+                x0_t[m + 1] = load_rows(x0, m + 1, "x0_")
             c1_t[m] = load_rows(c1, m, "c1_")
-            if m + 2 < TILES:
-                x0_t[m + 2] = load_rows(x0, m + 2, "x0_")
+        nc.sync.dma_start(out=d_rows[0:D_ROWS, :], in_=d[D_SPLIT:N].rearrange("(c p) -> c p", p=P))
         load_scales(1)
         for g in range(GROUPS):
             w_words[1, g] = load_words(1, g)
@@ -80,8 +90,8 @@ def tile_block_kaczmarz_sweep_t2_kernel(
         load_scales(2)
         for g in range(GROUPS):
             w_words[2, g] = load_words(2, g)
-        d_t = keep.tile([P, N], BF16, name="d_t")
-        nc.sync.dma_start(out=d_t[:], in_=d.partition_broadcast(P))
+        d_t = keep.tile([P, D_SPLIT], BF16, name="d_t")
+        nc.sync.dma_start(out=d_t[:], in_=d[0:D_SPLIT].partition_broadcast(P))
 
         rounded, grouped, codes, scales, x_t = {}, {}, {}, {}, {}
 
@@ -119,7 +129,7 @@ def tile_block_kaczmarz_sweep_t2_kernel(
                 out=acc[:],
                 lhsT=codes[i, g].bitcast(FP8X4),
                 lhsT_scale=scales[i, g],
-                rhs=w_words[s, g][:, 2 * ch * CHUNK : 2 * (ch + 1) * CHUNK].bitcast(FP4X4),
+                rhs=w_words[s, ch][:, g, :].bitcast(FP4X4),
                 rhs_scale=w_scales[s][:, g, ch * CHUNK : (ch + 1) * CHUNK],
                 start=(g == 0),
                 stop=(g == GROUPS - 1),
@@ -129,38 +139,56 @@ def tile_block_kaczmarz_sweep_t2_kernel(
         quantize(0)
         for i in range(STEPS):
             s, m = divmod(i, TILES)
-            accs = []
-            for ch in range(GROUPS):
-                acc = psum.tile([P, CHUNK], F32, name="acc", bufs=6)
-                accs.append(acc)
-            first = 0
-            if i == 0:
-                for ch in range(GROUPS):
-                    mx_pass(i, accs[ch], ch, 0)
-                turn(1)
-                quantize(1)
-                first = 1
-            for ch in range(GROUPS):
-                for g in range(first, GROUPS):
-                    mx_pass(i, accs[ch], ch, g)
-            if i + 2 < STEPS:
-                turn(i + 2)
-
-            minuend = (c1_t[m], c2_t[m], x_t.get(i - TILES))[s]
-            other = (x0_t[m], x_t.get(i - TILES), d_t)[s]
-            op = ALU.mult if s == STAGES - 1 else ALU.add
-            diff = work.tile([P, N], F32, name="diff")
             res = keep.tile([P, N], F32, name="res%d" % i)
             x_t[i] = res
+            if i == 0:
+                minuend = work.tile([P, N], F32, name="diff")
+                nc.vector.tensor_tensor(out=minuend[:], in0=x0_t[0][:], in1=c1_t[0][:], op=ALU.add)
+                diff = res
+            else:
+                minuend = (c1_t[m], c2_t[m], x_t.get(i - TILES))[s]
+                diff = work.tile([P, N], F32, name="diff")
             for ch in range(GROUPS):
+                acc = psum.tile([P, CHUNK], F32, name="acc", bufs=5)
+                for g in range(GROUPS):
+                    mx_pass(i, acc, ch, g)
                 cols = slice(ch * CHUNK, (ch + 1) * CHUNK)
-                nc.vector.tensor_tensor(out=diff[:, cols], in0=minuend[:, cols], in1=accs[ch][:], op=ALU.subtract)
-            for ch in range(GROUPS):
-                cols = slice(ch * CHUNK, (ch + 1) * CHUNK)
-                eng = nc.gpsimd if ch == 0 else nc.vector
-                eng.tensor_tensor(out=res[:, cols], in0=diff[:, cols], in1=other[:, cols], op=op)
-                if s == STAGES - 1:
-                    nc.sync.dma_start(out=out[m * P : (m + 1) * P, cols], in_=res[:, cols])
+                nc.vector.tensor_tensor(out=diff[:, cols], in0=minuend[:, cols], in1=acc[:], op=ALU.subtract)
+                if i == 0 and ch == 0:
+                    turn(1)
+                    quantize(1)
+            if i + 2 < STEPS:
+                turn(i + 2)
+            if i == TILES:
+                d_turn = psum.tile([P, P], BF16, name="d_bank")
+                nc.tensor.transpose(d_turn[:], d_rows[:], identity_bf[:])
+                d_cols = keep.tile([P, 8], BF16, name="d_cols")
+                nc.scalar.copy(out=d_cols[:], in_=d_turn[:, 0:8])
+            if i == TILES + 1:
+                d_spread = psum.tile([P, D_ROWS * P], BF16, name="d_bank")
+                for c in range(D_ROWS):
+                    nc.tensor.transpose(
+                        d_spread[:, c * P : (c + 1) * P], d_cols[:, c : c + 1].to_broadcast([P, P]), identity_bf[:]
+                    )
+
+            rows = slice(m * P, (m + 1) * P)
+            if s == STAGES - 1:
+                for lo, hi in ((0, CHUNK), (CHUNK, D_SPLIT)):
+                    nc.gpsimd.tensor_tensor(out=res[:, lo:hi], in0=diff[:, lo:hi], in1=d_t[:, lo:hi], op=ALU.mult)
+                for lo, hi in ((D_SPLIT, 2 * CHUNK), (2 * CHUNK, N)):
+                    nc.vector.tensor_tensor(
+                        out=res[:, lo:hi],
+                        in0=diff[:, lo:hi],
+                        in1=d_spread[:, lo - D_SPLIT : hi - D_SPLIT],
+                        op=ALU.mult,
+                    )
+                for ch in range(GROUPS):
+                    cols = slice(ch * CHUNK, (ch + 1) * CHUNK)
+                    nc.sync.dma_start(out=out[rows, cols], in_=res[:, cols])
+            elif i > 0:
+                other = x0_t[m] if s == 0 else x_t[i - TILES]
+                nc.gpsimd.tensor_tensor(out=res[:, 0:CHUNK], in0=diff[:, 0:CHUNK], in1=other[:, 0:CHUNK], op=ALU.add)
+                nc.vector.tensor_tensor(out=res[:, CHUNK:N], in0=diff[:, CHUNK:N], in1=other[:, CHUNK:N], op=ALU.add)
             if i + 2 < STEPS:
                 quantize(i + 2)
             if s < STAGES - 1:

@@ -22,7 +22,8 @@ TILES = M // P
 STAGES = 3
 STEPS = STAGES * TILES
 PARTS = ((0, 1), (1, 2))
-D_SPLIT = 768
+D_SPLIT = 512
+ADD_SPLIT = 384
 D_ROWS = (N - D_SPLIT) // P
 
 
@@ -71,9 +72,9 @@ def tile_block_kaczmarz_sweep_t2_kernel(
 
         x0_t, c1_t, c2_t, w_words = {}, {}, {}, {}
         x0_t[0] = load_rows(x0, 0, "x0_")
+        x0_t[1] = load_rows(x0, 1, "x0_")
         w_words[0, 0] = load_words(0, 0)
         load_scales(0)
-        x0_t[1] = load_rows(x0, 1, "x0_")
         c1_t[0] = load_rows(c1, 0, "c1_")
         w_words[0, 1] = load_words(0, 1)
         w_words[0, 2] = load_words(0, 2)
@@ -135,8 +136,9 @@ def tile_block_kaczmarz_sweep_t2_kernel(
                 stop=(g == GROUPS - 1),
             )
 
-        turn(0)
-        quantize(0)
+        for j in range(2):
+            turn(j)
+            quantize(j)
         for i in range(STEPS):
             s, m = divmod(i, TILES)
             res = keep.tile([P, N], F32, name="res%d" % i)
@@ -154,9 +156,6 @@ def tile_block_kaczmarz_sweep_t2_kernel(
                     mx_pass(i, acc, ch, g)
                 cols = slice(ch * CHUNK, (ch + 1) * CHUNK)
                 nc.vector.tensor_tensor(out=diff[:, cols], in0=minuend[:, cols], in1=acc[:], op=ALU.subtract)
-                if i == 0 and ch == 0:
-                    turn(1)
-                    quantize(1)
             if i + 2 < STEPS:
                 turn(i + 2)
             if i == TILES:
@@ -173,8 +172,7 @@ def tile_block_kaczmarz_sweep_t2_kernel(
 
             rows = slice(m * P, (m + 1) * P)
             if s == STAGES - 1:
-                for lo, hi in ((0, CHUNK), (CHUNK, D_SPLIT)):
-                    nc.gpsimd.tensor_tensor(out=res[:, lo:hi], in0=diff[:, lo:hi], in1=d_t[:, lo:hi], op=ALU.mult)
+                nc.gpsimd.tensor_tensor(out=res[:, 0:D_SPLIT], in0=diff[:, 0:D_SPLIT], in1=d_t[:], op=ALU.mult)
                 for lo, hi in ((D_SPLIT, 2 * CHUNK), (2 * CHUNK, N)):
                     nc.vector.tensor_tensor(
                         out=res[:, lo:hi],
@@ -187,8 +185,8 @@ def tile_block_kaczmarz_sweep_t2_kernel(
                     nc.sync.dma_start(out=out[rows, cols], in_=res[:, cols])
             elif i > 0:
                 other = x0_t[m] if s == 0 else x_t[i - TILES]
-                nc.gpsimd.tensor_tensor(out=res[:, 0:CHUNK], in0=diff[:, 0:CHUNK], in1=other[:, 0:CHUNK], op=ALU.add)
-                nc.vector.tensor_tensor(out=res[:, CHUNK:N], in0=diff[:, CHUNK:N], in1=other[:, CHUNK:N], op=ALU.add)
+                for eng, lo, hi in ((nc.gpsimd, 0, ADD_SPLIT), (nc.vector, ADD_SPLIT, 2 * CHUNK), (nc.vector, 2 * CHUNK, N)):
+                    eng.tensor_tensor(out=res[:, lo:hi], in0=diff[:, lo:hi], in1=other[:, lo:hi], op=ALU.add)
             if i + 2 < STEPS:
                 quantize(i + 2)
             if s < STAGES - 1:

@@ -23,7 +23,8 @@ STAGES = 3
 STEPS = STAGES * TILES
 PARTS = ((0, 1), (1, 2))
 D_SPLIT = 512
-ADD_SPLIT = 384
+ADD_SPLIT = 512
+MUL_SPLIT = 768
 D_ROWS = (N - D_SPLIT) // P
 
 
@@ -91,8 +92,8 @@ def tile_block_kaczmarz_sweep_t2_kernel(
         load_scales(2)
         for g in range(GROUPS):
             w_words[2, g] = load_words(2, g)
-        d_t = keep.tile([P, D_SPLIT], BF16, name="d_t")
-        nc.sync.dma_start(out=d_t[:], in_=d[0:D_SPLIT].partition_broadcast(P))
+        d_t = keep.tile([P, MUL_SPLIT], BF16, name="d_t")
+        nc.sync.dma_start(out=d_t[:], in_=d[0:MUL_SPLIT].partition_broadcast(P))
 
         rounded, grouped, codes, scales, x_t = {}, {}, {}, {}, {}
 
@@ -172,8 +173,11 @@ def tile_block_kaczmarz_sweep_t2_kernel(
 
             rows = slice(m * P, (m + 1) * P)
             if s == STAGES - 1:
-                nc.gpsimd.tensor_tensor(out=res[:, 0:D_SPLIT], in0=diff[:, 0:D_SPLIT], in1=d_t[:], op=ALU.mult)
-                for lo, hi in ((D_SPLIT, 2 * CHUNK), (2 * CHUNK, N)):
+                split = MUL_SPLIT if i + 1 < STEPS else CHUNK
+                for lo in range(0, split, CHUNK):
+                    hi = min(lo + CHUNK, split)
+                    nc.gpsimd.tensor_tensor(out=res[:, lo:hi], in0=diff[:, lo:hi], in1=d_t[:, lo:hi], op=ALU.mult)
+                for lo, hi in ((split, 2 * CHUNK), (2 * CHUNK, N)):
                     nc.vector.tensor_tensor(
                         out=res[:, lo:hi],
                         in0=diff[:, lo:hi],
@@ -193,9 +197,9 @@ def tile_block_kaczmarz_sweep_t2_kernel(
                 for part, (g0, ng) in enumerate(PARTS):
                     t = work.tile([P, ng * CHUNK], BF16, name="rounded%d" % part)
                     nc.scalar.copy(
-                        out=t[:].rearrange("p (g u q e) -> p g u q e", g=ng, u=2, e=2),
+                        out=t[:].rearrange("p (g u q e) -> p g q u e", g=ng, u=2, e=2),
                         in_=res[:, g0 * CHUNK : (g0 + ng) * CHUNK].rearrange(
-                            "p (g q u e) -> p g u q e", g=ng, u=2, e=2
+                            "p (g q u e) -> p g q u e", g=ng, u=2, e=2
                         ),
                     )
                     rounded[i + TILES, part] = t

from contextlib import ExitStack

import concourse.mybir as mybir
from concourse.masks import make_identity

M, N = 512, 1536
FLOPS = 3 * 2 * M * N * N

F32 = mybir.dt.float32
BF16 = mybir.dt.bfloat16
I32 = mybir.dt.int32
U32 = mybir.dt.uint32
U8 = mybir.dt.uint8
FP8X4 = mybir.dt.float8_e4m3fn_x4
FP4X4 = mybir.dt.float4_e2m1fn_x4
ALU = mybir.AluOpType

P = 128
CHUNK = 512
GROUPS = N // CHUNK
TILES = M // P
STAGES = 3
STEPS = STAGES * TILES
PARTS = ((0, 1), (1, 2))
D_SPLIT = 512
ADD_SPLIT = 512
MUL_SPLIT = 768
D_ROWS = (N - D_SPLIT) // P


def tile_block_kaczmarz_sweep_t2_kernel(
    tc, x0, c1, c2, d, proj1_words, proj1_scales, proj2_words, proj2_scales, proj3_words, proj3_scales, out
):
    nc = tc.nc
    words_hbm = (proj1_words, proj2_words, proj3_words)
    scales_hbm = (proj1_scales, proj2_scales, proj3_scales)

    with ExitStack() as ctx:
        keep = ctx.enter_context(tc.tile_pool(name="keep", bufs=1))
        work = ctx.enter_context(tc.tile_pool(name="work", bufs=3))
        psum = ctx.enter_context(tc.psum_pool(name="psum", bufs=1))
        ctx.enter_context(tc.manual_schedule())

        identity = keep.tile([P, P], F32, name="identity")
        make_identity(nc, identity[:])

        w_scales = []
        for s in range(STAGES):
            plane = keep.tile([P, GROUPS, N], U8, name="w_scales%d" % s, align_bytes=64)
            nc.vector.memset(plane[:].bitcast(I32), 0)
            w_scales.append(plane)

        identity_bf = keep.tile([P, P], BF16, name="identity_bf")
        nc.scalar.copy(out=identity_bf[:], in_=identity[:])
        d_rows = keep.tile([P, P], BF16, name="d_rows")
        nc.vector.memset(d_rows[:], 0.0)

        def load_rows(src, m, label):
            t = keep.tile([P, N], BF16, name="%s%d" % (label, m))
            nc.sync.dma_start(out=t[:], in_=src[m * P : (m + 1) * P, :])
            return t

        def load_words(s, ch):
            t = keep.tile([P, GROUPS, 2 * CHUNK], U8, name="w_words%d_%d" % (s, ch), align_bytes=64)
            src = words_hbm[s].bitcast(I32).rearrange("g p n -> p g n")
            nc.sync.dma_start(out=t[:].bitcast(I32), in_=src[:, :, ch * CHUNK // 2 : (ch + 1) * CHUNK // 2])
            return t

        def load_scales(s):
            rows = scales_hbm[s].bitcast(I32).rearrange("g (q r) n -> r q g n", r=4)
            for r in range(4):
                nc.sync.dma_start(out=w_scales[s][:].bitcast(I32)[r:P:32], in_=rows[r])

        x0_t, c1_t, c2_t, w_words = {}, {}, {}, {}
        x0_t[0] = load_rows(x0, 0, "x0_")
        x0_t[1] = load_rows(x0, 1, "x0_")
        w_words[0, 0] = load_words(0, 0)
        load_scales(0)
        c1_t[0] = load_rows(c1, 0, "c1_")
        w_words[0, 1] = load_words(0, 1)
        w_words[0, 2] = load_words(0, 2)
        for m in range(1, TILES):
            if m + 1 < TILES:
                x0_t[m + 1] = load_rows(x0, m + 1, "x0_")
            c1_t[m] = load_rows(c1, m, "c1_")
        nc.sync.dma_start(out=d_rows[0:D_ROWS, :], in_=d[D_SPLIT:N].rearrange("(c p) -> c p", p=P))
        load_scales(1)
        for g in range(GROUPS):
            w_words[1, g] = load_words(1, g)
        for m in range(TILES):
            c2_t[m] = load_rows(c2, m, "c2_")
        load_scales(2)
        for g in range(GROUPS):
            w_words[2, g] = load_words(2, g)
        d_t = keep.tile([P, MUL_SPLIT], BF16, name="d_t")
        nc.sync.dma_start(out=d_t[:], in_=d[0:MUL_SPLIT].partition_broadcast(P))

        rounded, grouped, codes, scales, x_t = {}, {}, {}, {}, {}

        def turn(j):
            for part, (g0, ng) in enumerate(PARTS):
                bank = psum.tile([P, ng, 2, P], F32, name="turn%d" % part)
                for gl in range(ng):
                    for u in range(2):
                        if j < TILES:
                            base = 256 * (g0 + gl)
                            src = x0_t[j][:].bitcast(F32)[:, base + u : base + 256 : 2]
                        else:
                            base = 256 * gl + P * u
                            src = rounded[j, part][:].bitcast(F32)[:, base : base + P]
                        nc.tensor.transpose(bank[:, gl, u, :], src, identity[:])
                t = work.tile([P, ng * CHUNK], BF16, name="grouped%d" % part, align_bytes=64)
                nc.scalar.copy(
                    out=t[:].bitcast(F32).rearrange("p (g m u) -> p g m u", g=ng, u=2),
                    in_=bank[:].rearrange("p g u m -> p g m u"),
                )
                grouped[j, part] = t

        def quantize(j):
            for part, (g0, ng) in enumerate(PARTS):
                cw = work.tile([P, ng * P], U32, name="codes%d" % part, align_bytes=64)
                sc = work.tile([P, ng * P], U8, name="scales%d" % part, align_bytes=64)
                nc.vector.quantize_mx(out=cw[:].bitcast(FP8X4), scales=sc[:], in_=grouped[j, part][:])
                for gl in range(ng):
                    codes[j, g0 + gl] = cw[:, gl * P : (gl + 1) * P]
                    scales[j, g0 + gl] = sc[:, gl * P : (gl + 1) * P]

        def mx_pass(i, acc, ch, g):
            s = i // TILES
            nc.tensor.matmul_mx(
                out=acc[:],
                lhsT=codes[i, g].bitcast(FP8X4),
                lhsT_scale=scales[i, g],
                rhs=w_words[s, ch][:, g, :].bitcast(FP4X4),
                rhs_scale=w_scales[s][:, g, ch * CHUNK : (ch + 1) * CHUNK],
                start=(g == 0),
                stop=(g == GROUPS - 1),
            )

        for j in range(2):
            turn(j)
            quantize(j)
        for i in range(STEPS):
            s, m = divmod(i, TILES)
            res = keep.tile([P, N], F32, name="res%d" % i)
            x_t[i] = res
            if i == 0:
                minuend = work.tile([P, N], F32, name="diff")
                nc.vector.tensor_tensor(out=minuend[:], in0=x0_t[0][:], in1=c1_t[0][:], op=ALU.add)
                diff = res
            else:
                minuend = (c1_t[m], c2_t[m], x_t.get(i - TILES))[s]
                diff = work.tile([P, N], F32, name="diff")
            for ch in range(GROUPS):
                acc = psum.tile([P, CHUNK], F32, name="acc", bufs=5)
                for g in range(GROUPS):
                    mx_pass(i, acc, ch, g)
                cols = slice(ch * CHUNK, (ch + 1) * CHUNK)
                nc.vector.tensor_tensor(out=diff[:, cols], in0=minuend[:, cols], in1=acc[:], op=ALU.subtract)
            if i + 2 < STEPS:
                turn(i + 2)
            if i == TILES:
                d_turn = psum.tile([P, P], BF16, name="d_bank")
                nc.tensor.transpose(d_turn[:], d_rows[:], identity_bf[:])
                d_cols = keep.tile([P, 8], BF16, name="d_cols")
                nc.scalar.copy(out=d_cols[:], in_=d_turn[:, 0:8])
            if i == TILES + 1:
                d_spread = psum.tile([P, D_ROWS * P], BF16, name="d_bank")
                for c in range(D_ROWS):
                    nc.tensor.transpose(
                        d_spread[:, c * P : (c + 1) * P], d_cols[:, c : c + 1].to_broadcast([P, P]), identity_bf[:]
                    )

            rows = slice(m * P, (m + 1) * P)
            if s == STAGES - 1:
                split = MUL_SPLIT if i + 1 < STEPS else CHUNK
                for lo in range(0, split, CHUNK):
                    hi = min(lo + CHUNK, split)
                    nc.gpsimd.tensor_tensor(out=res[:, lo:hi], in0=diff[:, lo:hi], in1=d_t[:, lo:hi], op=ALU.mult)
                for lo, hi in ((split, 2 * CHUNK), (2 * CHUNK, N)):
                    nc.vector.tensor_tensor(
                        out=res[:, lo:hi],
                        in0=diff[:, lo:hi],
                        in1=d_spread[:, lo - D_SPLIT : hi - D_SPLIT],
                        op=ALU.mult,
                    )
                for ch in range(GROUPS):
                    cols = slice(ch * CHUNK, (ch + 1) * CHUNK)
                    nc.sync.dma_start(out=out[rows, cols], in_=res[:, cols])
            elif i > 0:
                other = x0_t[m] if s == 0 else x_t[i - TILES]
                for eng, lo, hi in ((nc.gpsimd, 0, ADD_SPLIT), (nc.vector, ADD_SPLIT, 2 * CHUNK), (nc.vector, 2 * CHUNK, N)):
                    eng.tensor_tensor(out=res[:, lo:hi], in0=diff[:, lo:hi], in1=other[:, lo:hi], op=ALU.add)
            if i + 2 < STEPS:
                quantize(i + 2)
            if s < STAGES - 1:
                for part, (g0, ng) in enumerate(PARTS):
                    t = work.tile([P, ng * CHUNK], BF16, name="rounded%d" % part)
                    nc.scalar.copy(
                        out=t[:].rearrange("p (g u q e) -> p g q u e", g=ng, u=2, e=2),
                        in_=res[:, g0 * CHUNK : (g0 + ng) * CHUNK].rearrange(
                            "p (g q u e) -> p g q u e", g=ng, u=2, e=2
                        ),
                    )
                    rounded[i + TILES, part] = t
